import numpy as np
import ml_dtypes


def mxq(x, axis, fmt="e4m3"):
    dtype, down = {"e4m3": (ml_dtypes.float8_e4m3fn, 7), "e5m2": (ml_dtypes.float8_e5m2, 14)}[fmt]
    v = np.moveaxis(np.asarray(x, np.float32).astype(ml_dtypes.bfloat16).astype(np.float64), axis, -1)
    blocks = v.reshape(v.shape[:-1] + (-1, 32))
    amax = np.abs(blocks).max(-1, keepdims=True)
    byte = np.maximum(np.where(amax > 0, np.frexp(amax)[1] - 1 + 127, 0) - down, 1)
    scale = np.exp2(byte - 127.0)
    codes = (blocks / scale).astype(np.float32).astype(dtype).astype(np.float64)
    return np.moveaxis((codes * scale).reshape(v.shape), -1, axis)


WIDE = False


def mx_kscale(k):
    if not WIDE:
        return np.ones(k)
    levels = np.array([10, -10, 5, -5, 0])
    if k % 512:
        return np.exp2(np.random.permutation(np.resize(levels, k // 32))).repeat(32)
    a = np.empty((k // 512, 16))
    for p in range(k // 512):
        a[p, :8] = np.random.permutation(np.resize(levels, 8))
        for g in range(8):
            far = levels[np.abs(levels - a[p, g]) >= 10]
            a[p, g + 8] = far[np.random.randint(len(far))]
    return np.exp2(a.ravel()).repeat(32)


def f64(x):
    return np.asarray(x).astype(np.float64)


def striped8(idx):
    return np.asarray(idx).reshape(8, -1, 16).transpose(0, 2, 1).reshape(128, -1).astype(np.uint16)


def unstriped8(offs):
    return offs.reshape(8, 16, -1).transpose(0, 2, 1).reshape(8, -1).astype(np.int64)


def pick8(x, idx, run):
    r = np.arange(len(x))
    return x[r[:, None], idx[r % (8 * run) // run]]


E2M1 = np.array([0.0, 0.5, 1.0, 1.5, 2.0, 3.0, 4.0, 6.0, -0.0, -0.5, -1.0, -1.5, -2.0, -3.0, -4.0, -6.0])


def pack_weight(w, fmt):
    k, n = w.shape
    w = f64(np.asarray(w, np.float32).astype(ml_dtypes.bfloat16)).reshape(k // 32, 32, n)
    amax = np.abs(w).max(1)
    if fmt == "e4m3":
        byte = np.frexp(amax)[1] - 1 + 127 - 7
    else:
        mant, ex = np.frexp(amax / 6.0)
        byte = np.where(mant > 0.5, ex, ex - 1) + 127
    byte = np.clip(np.where(amax > 0, byte, 1), 1, 254)
    scaled = (w * np.exp2(127.0 - byte)[:, None, :]).reshape(k, n).astype(np.float32)
    by_word = np.ascontiguousarray(scaled.reshape(k // 512, 128, 4, n).transpose(0, 1, 3, 2))
    if fmt == "e4m3":
        words = by_word.astype(ml_dtypes.float8_e4m3fn).view(np.uint8)
    else:
        c = by_word.astype(ml_dtypes.float4_e2m1fn).view(np.uint8) & 0xF
        words = (c[..., 0::2] | (c[..., 1::2] << 4)).reshape(k // 512, 128, 2 * n)
    return np.ascontiguousarray(words), np.ascontiguousarray(byte.astype(np.uint8).reshape(k // 512, 16, n))


def unpack_weight(words, scales, fmt):
    g, _, n = scales.shape
    words = np.ascontiguousarray(words).reshape(g, 128, n, -1)
    if fmt == "e4m3":
        vals = words.view(ml_dtypes.float8_e4m3fn).astype(np.float64)
    else:
        nib = np.empty((g, 128, n, 4), np.uint8)
        nib[..., 0::2] = words & 0xF
        nib[..., 1::2] = words >> 4
        vals = E2M1[nib]
    vals = vals * np.repeat(np.exp2(scales.astype(np.float64) - 127.0), 8, axis=1)[..., None]
    return vals.transpose(0, 1, 3, 2).reshape(g * 512, n)


def sigmoid(v):
    return 1.0 / (1.0 + np.exp(-v))


D, T, I, Q = 512, 1024, 512, 128


def setup_inputs():
    n = np.random.standard_normal
    idx = np.stack([np.random.permutation(T)[:I] for _ in range(8)])
    idx2 = np.stack([np.random.permutation(T)[:I] for _ in range(8)])
    idx3 = np.stack([np.random.permutation(T)[:I] for _ in range(8)])
    idx4 = np.stack([np.random.permutation(T)[:I] for _ in range(8)])
    fd = mx_kscale(D)
    keysp = pack_weight(n((D, T)) / fd[:, None], "e4m3")
    return {
        "query": (n((D, Q)) * 1.2 / np.sqrt(D) * fd[:, None]).astype(np.float32),
        "keys_words": keysp[0],
        "keys_scales": keysp[1],
        "lam": (np.random.uniform(0.5, 1.5, (Q, 1))).astype(np.float32),
        "old": (1.0 * n((Q, T))).astype(np.float32),
        "share2": (np.random.uniform(0.4, 1.2, (Q, 1))).astype(np.float32),
        "offs": striped8(idx),
        "offs2": striped8(idx2),
        "offs3": striped8(idx3),
        "offs4": striped8(idx4),
    }


def reference(query, keys_words, keys_scales, lam, old, share2, offs, offs2, offs3, offs4):
    idx = unstriped8(offs)
    idx2 = unstriped8(offs2)
    idx3 = unstriped8(offs3)
    idx4 = unstriped8(offs4)
    keysu = unpack_weight(keys_words, keys_scales, "e4m3")
    queryq = mxq(f64(query), 0, "e4m3")
    a = queryq.T @ keysu
    g1 = sigmoid(pick8(a, idx2, 16) * 2.0)
    w = (pick8(a, idx, 16) * g1 + pick8(a, idx3, 16) * (1.0 - g1)) * f64(lam)
    f1 = np.zeros((Q, T))
    f1[np.arange(Q)[:, None], idx[np.arange(Q) % 128 // 16]] = w
    f2 = np.zeros((Q, T))
    f2[np.arange(Q)[:, None], idx4[np.arange(Q) % 128 // 16]] = w
    y = f64(old) + f1 + f2 * f64(share2)
    return y

@@ -1,0 +1,167 @@
+from contextlib import ExitStack
+
+import concourse.mybir as mybir
+from concourse.masks import make_identity
+
+D, T, I, Q = 512, 1024, 512, 128
+FLOPS = 2 * D * Q * T
+
+F32 = mybir.dt.float32
+BF16 = mybir.dt.bfloat16
+I32 = mybir.dt.int32
+U32 = mybir.dt.uint32
+U16 = mybir.dt.uint16
+U8 = mybir.dt.uint8
+FP8X4 = mybir.dt.float8_e4m3fn_x4
+ALU = mybir.AluOpType
+ACT = mybir.ActivationFunctionType
+
+P = 128
+PACK = 4
+GROUP = 16
+HALF = I // 2
+MM_N = 256
+LOAD_N = 512
+BANK = 512
+OUT_N = 256
+
+
+def tile_attend_conditioned_lean_twiceput_heads_kernel(
+    tc, query, keys_words, keys_scales, lam, old, share2, offs, offs2, offs3, offs4, out
+):
+    nc = tc.nc
+    with ExitStack() as ctx:
+        lists = ctx.enter_context(tc.tile_pool(name="lists", bufs=1))
+        sb = ctx.enter_context(tc.tile_pool(name="sb", bufs=1))
+        psum = ctx.enter_context(tc.psum_pool(name="psum", bufs=1))
+
+        q_raw = sb.tile([P, PACK, Q], F32, name="q_raw")
+        nc.sync.dma_start(out=q_raw[:], in_=query.rearrange("(p j) q -> p j q", j=PACK))
+
+        judge = lists.tile([P, I // GROUP], U16, name="judge")
+        nc.sync.dma_start(judge[:], offs2)
+
+        k_scales = sb.tile([P, T], U8, name="k_scales", align_bytes=64)
+        for quad in range(4):
+            nc.sync.dma_start(
+                out=k_scales[32 * quad : 32 * quad + 4, :].bitcast(I32),
+                in_=keys_scales[0, 4 * quad : 4 * quad + 4, :].bitcast(I32),
+            )
+        words_hbm = keys_words[0].rearrange("p n t -> p (n t)")
+        k_words = []
+        for c in range(T // LOAD_N):
+            part = sb.tile([P, LOAD_N], U32, name="k_words%d" % c, align_bytes=64)
+            nc.sync.dma_start(
+                out=part[:].bitcast(I32),
+                in_=words_hbm[:, c * LOAD_N * PACK : (c + 1) * LOAD_N * PACK].bitcast(I32),
+            )
+            k_words.append(part)
+
+        first = lists.tile([P, I // GROUP], U16, name="first")
+        second = lists.tile([P, I // GROUP], U16, name="second")
+        extra = lists.tile([P, I // GROUP], U16, name="extra")
+        nc.sync.dma_start(first[:], offs)
+        nc.sync.dma_start(second[:], offs3)
+        lam_sb = sb.tile([P, 1], F32, name="lam_sb")
+        nc.sync.dma_start(out=lam_sb[:], in_=lam)
+        nc.sync.dma_start(extra[:], offs4)
+        share_sb = sb.tile([P, 1], F32, name="share_sb")
+        nc.sync.dma_start(out=share_sb[:], in_=share2)
+        old_sb = sb.tile([P, T], F32, name="old_sb")
+        nc.sync.dma_start(out=old_sb[:], in_=old)
+
+        f1 = sb.tile([P, T], F32, name="f1")
+        f2 = sb.tile([P, T], F32, name="f2")
+        nc.vector.memset(f1[:], 0.0)
+        nc.vector.memset(f2[:], 0.0)
+        ident = sb.tile([P, P], F32, name="ident")
+        make_identity(nc, ident[:])
+
+        q_bf = sb.tile([P, Q, PACK], BF16, name="q_bf", align_bytes=64)
+        nc.vector.tensor_copy(out=q_bf[:], in_=q_raw[:].rearrange("p j q -> p q j"))
+        q_words = sb.tile([P, Q], U32, name="q_words", align_bytes=64)
+        q_scales = sb.tile([P, Q], U8, name="q_scales", align_bytes=64)
+        nc.vector.quantize_mx(
+            out=q_words[:].bitcast(FP8X4),
+            scales=q_scales[:],
+            in_=q_bf[:].rearrange("p q j -> p (q j)"),
+        )
+
+        a = sb.tile([P, T], F32, name="a")
+        for c in range(T // MM_N):
+            cols = slice(c * MM_N, (c + 1) * MM_N)
+            part, off = divmod(c * MM_N, LOAD_N)
+            acc = psum.tile([P, MM_N], F32, name="acc%d" % c)
+            nc.tensor.matmul_mx(
+                out=acc[:],
+                lhsT=q_words[:].bitcast(FP8X4),
+                lhsT_scale=q_scales[:],
+                rhs=k_words[part][:, off : off + MM_N].bitcast(FP8X4),
+                rhs_scale=k_scales[:, cols],
+                start=True,
+                stop=True,
+            )
+            nc.vector.tensor_copy(out=a[:, cols], in_=acc[:])
+
+        turned = [psum.tile([P, BANK], F32, name="turned%d" % b) for b in range(T // BANK)]
+        for blk in range(T // P):
+            b, j = divmod(blk, BANK // P)
+            nc.tensor.matmul(
+                turned[b][:, j * P : (j + 1) * P],
+                old_sb[:, blk * P : (blk + 1) * P],
+                ident[:],
+                start=(j == 0),
+                stop=False,
+                is_transpose=True,
+            )
+
+        w_first = sb.tile([P, I], F32, name="w_first")
+        w_second = sb.tile([P, I], F32, name="w_second")
+        for h in range(2):
+            slots = slice(h * HALF, (h + 1) * HALF)
+            ocols = slice(h * HALF // GROUP, (h + 1) * HALF // GROUP)
+            gate = sb.tile([P, HALF], F32, name="gate%d" % h)
+            rest = sb.tile([P, HALF], F32, name="rest%d" % h)
+            a1 = sb.tile([P, HALF], F32, name="a1_%d" % h)
+            a3 = sb.tile([P, HALF], F32, name="a3_%d" % h)
+            nc.scalar.activation(gate[:], a[:].indirect(judge[:, ocols]), ACT.Sigmoid, scale=2.0)
+            if h == 0:
+                nc.vector.tensor_copy(a1[:], a[:].indirect(first[:, ocols]))
+                nc.vector.tensor_copy(a3[:], a[:].indirect(second[:, ocols]))
+                nc.scalar.activation(rest[:], gate[:], ACT.Copy, bias=1.0, scale=-1.0)
+            else:
+                nc.scalar.activation(a1[:], a[:].indirect(first[:, ocols]), ACT.Copy)
+                nc.scalar.activation(rest[:], gate[:], ACT.Copy, bias=1.0, scale=-1.0)
+                nc.scalar.activation(a3[:], a[:].indirect(second[:, ocols]), ACT.Copy)
+            nc.vector.scalar_tensor_tensor(w_first[:, slots], a1[:], lam_sb[:], gate[:], ALU.mult, ALU.mult)
+            nc.vector.scalar_tensor_tensor(w_second[:, slots], a3[:], lam_sb[:], rest[:], ALU.mult, ALU.mult)
+            nc.vector.tensor_tensor(f1[:].indirect(first[:, ocols]), w_first[:, slots], w_second[:, slots], ALU.add)
+        nc.vector.tensor_tensor(f2[:].indirect(extra[:]), w_first[:], w_second[:], ALU.add)
+
+        for blk in range(T // P):
+            b, j = divmod(blk, BANK // P)
+            nc.tensor.matmul(
+                turned[b][:, j * P : (j + 1) * P],
+                f1[:, blk * P : (blk + 1) * P],
+                ident[:],
+                start=False,
+                stop=(j == BANK // P - 1),
+                is_transpose=True,
+            )
+        back = []
+        for b in range(T // BANK):
+            turned_sb = sb.tile([P, BANK], F32, name="turned_sb%d" % b)
+            nc.scalar.copy(turned_sb[:], turned[b][:])
+            bank = psum.tile([P, BANK], F32, name="back%d" % b)
+            for j in range(BANK // P):
+                nc.tensor.transpose(bank[:, j * P : (j + 1) * P], turned_sb[:, j * P : (j + 1) * P], ident[:])
+            back.append(bank)
+
+        for c in range(T // OUT_N):
+            cols = slice(c * OUT_N, (c + 1) * OUT_N)
+            b, off = divmod(c * OUT_N, BANK)
+            res = sb.tile([P, OUT_N], F32, name="res%d" % c)
+            nc.vector.scalar_tensor_tensor(
+                res[:], f2[:, cols], share_sb[:], back[b][:, off : off + OUT_N], ALU.mult, ALU.add
+            )
+            nc.sync.dma_start(out=out[:, cols], in_=res[:])

@@ -22,8 +22,8 @@ GROUP = 16
 HALF = I // 2
 MM_N = 256
 LOAD_N = 512
-BANK = 512
-OUT_N = 256
+BANK = 256
+OUT_WIDTHS = (256, 256, 256, 128, 128)
 
 
 def tile_attend_conditioned_lean_twiceput_heads_kernel(
@@ -78,20 +78,26 @@ def tile_attend_conditioned_lean_twiceput_heads_kernel(
         make_identity(nc, ident[:])
 
         q_bf = sb.tile([P, Q, PACK], BF16, name="q_bf", align_bytes=64)
-        nc.vector.tensor_copy(out=q_bf[:], in_=q_raw[:].rearrange("p j q -> p q j"))
         q_words = sb.tile([P, Q], U32, name="q_words", align_bytes=64)
         q_scales = sb.tile([P, Q], U8, name="q_scales", align_bytes=64)
-        nc.vector.quantize_mx(
-            out=q_words[:].bitcast(FP8X4),
-            scales=q_scales[:],
-            in_=q_bf[:].rearrange("p q j -> p (q j)"),
-        )
+        q_halves = [slice(0, Q // 2), slice(Q // 2, Q)]
+        for rows in q_halves:
+            nc.vector.tensor_copy(
+                out=q_bf[:, rows, :].rearrange("p (c i) j -> p c j i", i=PACK),
+                in_=q_raw[:, :, rows].rearrange("p j (c i) -> p c j i", i=PACK),
+            )
+        for rows in q_halves:
+            nc.vector.quantize_mx(
+                out=q_words[:, rows].bitcast(FP8X4),
+                scales=q_scales[:, rows],
+                in_=q_bf[:, rows, :].rearrange("p q j -> p (q j)"),
+            )
 
         a = sb.tile([P, T], F32, name="a")
         for c in range(T // MM_N):
             cols = slice(c * MM_N, (c + 1) * MM_N)
             part, off = divmod(c * MM_N, LOAD_N)
-            acc = psum.tile([P, MM_N], F32, name="acc%d" % c)
+            acc = psum.tile([P, MM_N], F32, name="acc%d" % c, tag="bank%d" % c)
             nc.tensor.matmul_mx(
                 out=acc[:],
                 lhsT=q_words[:].bitcast(FP8X4),
@@ -122,19 +128,20 @@ def tile_attend_conditioned_lean_twiceput_heads_kernel(
             ocols = slice(h * HALF // GROUP, (h + 1) * HALF // GROUP)
             gate = sb.tile([P, HALF], F32, name="gate%d" % h)
             rest = sb.tile([P, HALF], F32, name="rest%d" % h)
-            a1 = sb.tile([P, HALF], F32, name="a1_%d" % h)
-            a3 = sb.tile([P, HALF], F32, name="a3_%d" % h)
+            cand = sb.tile([P, 2 * HALF], F32, name="cand%d" % h, tag="cand")
+            a1 = cand[:, 0:HALF]
+            a3 = cand[:, HALF : 2 * HALF]
             nc.scalar.activation(gate[:], a[:].indirect(judge[:, ocols]), ACT.Sigmoid, scale=2.0)
             if h == 0:
-                nc.vector.tensor_copy(a1[:], a[:].indirect(first[:, ocols]))
-                nc.vector.tensor_copy(a3[:], a[:].indirect(second[:, ocols]))
-                nc.scalar.activation(rest[:], gate[:], ACT.Copy, bias=1.0, scale=-1.0)
+                nc.scalar.activation(rest[:], a[:].indirect(judge[:, ocols]), ACT.Sigmoid, scale=-2.0)
+                nc.vector.tensor_copy(a1, a[:].indirect(first[:, ocols]))
+                nc.vector.tensor_copy(a3, a[:].indirect(second[:, ocols]))
             else:
-                nc.scalar.activation(a1[:], a[:].indirect(first[:, ocols]), ACT.Copy)
                 nc.scalar.activation(rest[:], gate[:], ACT.Copy, bias=1.0, scale=-1.0)
-                nc.scalar.activation(a3[:], a[:].indirect(second[:, ocols]), ACT.Copy)
-            nc.vector.scalar_tensor_tensor(w_first[:, slots], a1[:], lam_sb[:], gate[:], ALU.mult, ALU.mult)
-            nc.vector.scalar_tensor_tensor(w_second[:, slots], a3[:], lam_sb[:], rest[:], ALU.mult, ALU.mult)
+                nc.scalar.activation(a1, a[:].indirect(first[:, ocols]), ACT.Copy)
+                nc.scalar.activation(a3, a[:].indirect(second[:, ocols]), ACT.Copy)
+            nc.vector.scalar_tensor_tensor(w_first[:, slots], a1, lam_sb[:], gate[:], ALU.mult, ALU.mult)
+            nc.vector.scalar_tensor_tensor(w_second[:, slots], a3, lam_sb[:], rest[:], ALU.mult, ALU.mult)
             nc.vector.tensor_tensor(f1[:].indirect(first[:, ocols]), w_first[:, slots], w_second[:, slots], ALU.add)
         nc.vector.tensor_tensor(f2[:].indirect(extra[:]), w_first[:], w_second[:], ALU.add)
 
@@ -152,16 +159,18 @@ def tile_attend_conditioned_lean_twiceput_heads_kernel(
         for b in range(T // BANK):
             turned_sb = sb.tile([P, BANK], F32, name="turned_sb%d" % b)
             nc.scalar.copy(turned_sb[:], turned[b][:])
-            bank = psum.tile([P, BANK], F32, name="back%d" % b)
+            bank = psum.tile([P, BANK], F32, name="back%d" % b, tag="bank%d" % b)
             for j in range(BANK // P):
                 nc.tensor.transpose(bank[:, j * P : (j + 1) * P], turned_sb[:, j * P : (j + 1) * P], ident[:])
             back.append(bank)
 
-        for c in range(T // OUT_N):
-            cols = slice(c * OUT_N, (c + 1) * OUT_N)
-            b, off = divmod(c * OUT_N, BANK)
-            res = sb.tile([P, OUT_N], F32, name="res%d" % c)
+        start = 0
+        for c, width in enumerate(OUT_WIDTHS):
+            cols = slice(start, start + width)
+            b, off = divmod(start, BANK)
+            res = sb.tile([P, width], F32, name="res%d" % c)
             nc.vector.scalar_tensor_tensor(
-                res[:], f2[:, cols], share_sb[:], back[b][:, off : off + OUT_N], ALU.mult, ALU.add
+                res[:], f2[:, cols], share_sb[:], back[b][:, off : off + width], ALU.mult, ALU.add
             )
             nc.sync.dma_start(out=out[:, cols], in_=res[:])
+            start = start + width

from contextlib import ExitStack

import concourse.mybir as mybir
from concourse.masks import make_identity

D, T, I, Q = 512, 1024, 512, 128
FLOPS = 2 * D * Q * T

F32 = mybir.dt.float32
BF16 = mybir.dt.bfloat16
I32 = mybir.dt.int32
U32 = mybir.dt.uint32
U16 = mybir.dt.uint16
U8 = mybir.dt.uint8
FP8X4 = mybir.dt.float8_e4m3fn_x4
ALU = mybir.AluOpType
ACT = mybir.ActivationFunctionType

P = 128
PACK = 4
GROUP = 16
HALF = I // 2
MM_N = 256
LOAD_N = 512
BANK = 256
OUT_WIDTHS = (256, 256, 256, 128, 128)


def tile_attend_conditioned_lean_twiceput_heads_kernel(
    tc, query, keys_words, keys_scales, lam, old, share2, offs, offs2, offs3, offs4, out
):
    nc = tc.nc
    with ExitStack() as ctx:
        lists = ctx.enter_context(tc.tile_pool(name="lists", bufs=1))
        sb = ctx.enter_context(tc.tile_pool(name="sb", bufs=1))
        psum = ctx.enter_context(tc.psum_pool(name="psum", bufs=1))

        q_raw = sb.tile([P, PACK, Q], F32, name="q_raw")
        nc.sync.dma_start(out=q_raw[:], in_=query.rearrange("(p j) q -> p j q", j=PACK))

        judge = lists.tile([P, I // GROUP], U16, name="judge")
        nc.sync.dma_start(judge[:], offs2)

        k_scales = sb.tile([P, T], U8, name="k_scales", align_bytes=64)
        for quad in range(4):
            nc.sync.dma_start(
                out=k_scales[32 * quad : 32 * quad + 4, :].bitcast(I32),
                in_=keys_scales[0, 4 * quad : 4 * quad + 4, :].bitcast(I32),
            )
        words_hbm = keys_words[0].rearrange("p n t -> p (n t)")
        k_words = []
        for c in range(T // LOAD_N):
            part = sb.tile([P, LOAD_N], U32, name="k_words%d" % c, align_bytes=64)
            nc.sync.dma_start(
                out=part[:].bitcast(I32),
                in_=words_hbm[:, c * LOAD_N * PACK : (c + 1) * LOAD_N * PACK].bitcast(I32),
            )
            k_words.append(part)

        first = lists.tile([P, I // GROUP], U16, name="first")
        second = lists.tile([P, I // GROUP], U16, name="second")
        extra = lists.tile([P, I // GROUP], U16, name="extra")
        nc.sync.dma_start(first[:], offs)
        nc.sync.dma_start(second[:], offs3)
        lam_sb = sb.tile([P, 1], F32, name="lam_sb")
        nc.sync.dma_start(out=lam_sb[:], in_=lam)
        nc.sync.dma_start(extra[:], offs4)
        share_sb = sb.tile([P, 1], F32, name="share_sb")
        nc.sync.dma_start(out=share_sb[:], in_=share2)
        old_sb = sb.tile([P, T], F32, name="old_sb")
        nc.sync.dma_start(out=old_sb[:], in_=old)

        f1 = sb.tile([P, T], F32, name="f1")
        f2 = sb.tile([P, T], F32, name="f2")
        nc.vector.memset(f1[:], 0.0)
        nc.vector.memset(f2[:], 0.0)
        ident = sb.tile([P, P], F32, name="ident")
        make_identity(nc, ident[:])

        q_bf = sb.tile([P, Q, PACK], BF16, name="q_bf", align_bytes=64)
        q_words = sb.tile([P, Q], U32, name="q_words", align_bytes=64)
        q_scales = sb.tile([P, Q], U8, name="q_scales", align_bytes=64)
        q_halves = [slice(0, Q // 2), slice(Q // 2, Q)]
        for rows in q_halves:
            nc.vector.tensor_copy(
                out=q_bf[:, rows, :].rearrange("p (c i) j -> p c j i", i=PACK),
                in_=q_raw[:, :, rows].rearrange("p j (c i) -> p c j i", i=PACK),
            )
        for rows in q_halves:
            nc.vector.quantize_mx(
                out=q_words[:, rows].bitcast(FP8X4),
                scales=q_scales[:, rows],
                in_=q_bf[:, rows, :].rearrange("p q j -> p (q j)"),
            )

        a = sb.tile([P, T], F32, name="a")
        for c in range(T // MM_N):
            cols = slice(c * MM_N, (c + 1) * MM_N)
            part, off = divmod(c * MM_N, LOAD_N)
            acc = psum.tile([P, MM_N], F32, name="acc%d" % c, tag="bank%d" % c)
            nc.tensor.matmul_mx(
                out=acc[:],
                lhsT=q_words[:].bitcast(FP8X4),
                lhsT_scale=q_scales[:],
                rhs=k_words[part][:, off : off + MM_N].bitcast(FP8X4),
                rhs_scale=k_scales[:, cols],
                start=True,
                stop=True,
            )
            nc.vector.tensor_copy(out=a[:, cols], in_=acc[:])

        turned = [psum.tile([P, BANK], F32, name="turned%d" % b) for b in range(T // BANK)]
        for blk in range(T // P):
            b, j = divmod(blk, BANK // P)
            nc.tensor.matmul(
                turned[b][:, j * P : (j + 1) * P],
                old_sb[:, blk * P : (blk + 1) * P],
                ident[:],
                start=(j == 0),
                stop=False,
                is_transpose=True,
            )

        w_first = sb.tile([P, I], F32, name="w_first")
        w_second = sb.tile([P, I], F32, name="w_second")
        for h in range(2):
            slots = slice(h * HALF, (h + 1) * HALF)
            ocols = slice(h * HALF // GROUP, (h + 1) * HALF // GROUP)
            gate = sb.tile([P, HALF], F32, name="gate%d" % h)
            rest = sb.tile([P, HALF], F32, name="rest%d" % h)
            cand = sb.tile([P, 2 * HALF], F32, name="cand%d" % h, tag="cand")
            a1 = cand[:, 0:HALF]
            a3 = cand[:, HALF : 2 * HALF]
            nc.scalar.activation(gate[:], a[:].indirect(judge[:, ocols]), ACT.Sigmoid, scale=2.0)
            if h == 0:
                nc.scalar.activation(rest[:], a[:].indirect(judge[:, ocols]), ACT.Sigmoid, scale=-2.0)
                nc.vector.tensor_copy(a1, a[:].indirect(first[:, ocols]))
                nc.vector.tensor_copy(a3, a[:].indirect(second[:, ocols]))
            else:
                nc.scalar.activation(rest[:], gate[:], ACT.Copy, bias=1.0, scale=-1.0)
                nc.scalar.activation(a1, a[:].indirect(first[:, ocols]), ACT.Copy)
                nc.scalar.activation(a3, a[:].indirect(second[:, ocols]), ACT.Copy)
            nc.vector.scalar_tensor_tensor(w_first[:, slots], a1, lam_sb[:], gate[:], ALU.mult, ALU.mult)
            nc.vector.scalar_tensor_tensor(w_second[:, slots], a3, lam_sb[:], rest[:], ALU.mult, ALU.mult)
            nc.vector.tensor_tensor(f1[:].indirect(first[:, ocols]), w_first[:, slots], w_second[:, slots], ALU.add)
        nc.vector.tensor_tensor(f2[:].indirect(extra[:]), w_first[:], w_second[:], ALU.add)

        for blk in range(T // P):
            b, j = divmod(blk, BANK // P)
            nc.tensor.matmul(
                turned[b][:, j * P : (j + 1) * P],
                f1[:, blk * P : (blk + 1) * P],
                ident[:],
                start=False,
                stop=(j == BANK // P - 1),
                is_transpose=True,
            )
        back = []
        for b in range(T // BANK):
            turned_sb = sb.tile([P, BANK], F32, name="turned_sb%d" % b)
            nc.scalar.copy(turned_sb[:], turned[b][:])
            bank = psum.tile([P, BANK], F32, name="back%d" % b, tag="bank%d" % b)
            for j in range(BANK // P):
                nc.tensor.transpose(bank[:, j * P : (j + 1) * P], turned_sb[:, j * P : (j + 1) * P], ident[:])
            back.append(bank)

        start = 0
        for c, width in enumerate(OUT_WIDTHS):
            cols = slice(start, start + width)
            b, off = divmod(start, BANK)
            res = sb.tile([P, width], F32, name="res%d" % c)
            nc.vector.scalar_tensor_tensor(
                res[:], f2[:, cols], share_sb[:], back[b][:, off : off + width], ALU.mult, ALU.add
            )
            nc.sync.dma_start(out=out[:, cols], in_=res[:])
            start = start + width
